import numpy as np
import ml_dtypes


def mxq(x, axis, fmt="e4m3"):
    dtype, down = {"e4m3": (ml_dtypes.float8_e4m3fn, 7), "e5m2": (ml_dtypes.float8_e5m2, 14)}[fmt]
    v = np.moveaxis(np.asarray(x, np.float32).astype(ml_dtypes.bfloat16).astype(np.float64), axis, -1)
    blocks = v.reshape(v.shape[:-1] + (-1, 32))
    amax = np.abs(blocks).max(-1, keepdims=True)
    byte = np.maximum(np.where(amax > 0, np.frexp(amax)[1] - 1 + 127, 0) - down, 1)
    scale = np.exp2(byte - 127.0)
    codes = (blocks / scale).astype(np.float32).astype(dtype).astype(np.float64)
    return np.moveaxis((codes * scale).reshape(v.shape), -1, axis)


WIDE = False


def mx_kscale(k):
    if not WIDE:
        return np.ones(k)
    levels = np.array([10, -10, 5, -5, 0])
    if k % 512:
        return np.exp2(np.random.permutation(np.resize(levels, k // 32))).repeat(32)
    a = np.empty((k // 512, 16))
    for p in range(k // 512):
        a[p, :8] = np.random.permutation(np.resize(levels, 8))
        for g in range(8):
            far = levels[np.abs(levels - a[p, g]) >= 10]
            a[p, g + 8] = far[np.random.randint(len(far))]
    return np.exp2(a.ravel()).repeat(32)


def f64(x):
    return np.asarray(x).astype(np.float64)


def striped(idx):
    return np.tile(np.asarray(idx).reshape(-1, 16).T, (8, 1)).astype(np.uint16)


def unstriped(offs):
    return offs[:16].T.reshape(-1).astype(np.int64)


E2M1 = np.array([0.0, 0.5, 1.0, 1.5, 2.0, 3.0, 4.0, 6.0, -0.0, -0.5, -1.0, -1.5, -2.0, -3.0, -4.0, -6.0])


def pack_weight(w, fmt):
    k, n = w.shape
    w = f64(np.asarray(w, np.float32).astype(ml_dtypes.bfloat16)).reshape(k // 32, 32, n)
    amax = np.abs(w).max(1)
    if fmt == "e4m3":
        byte = np.frexp(amax)[1] - 1 + 127 - 7
    else:
        mant, ex = np.frexp(amax / 6.0)
        byte = np.where(mant > 0.5, ex, ex - 1) + 127
    byte = np.clip(np.where(amax > 0, byte, 1), 1, 254)
    scaled = (w * np.exp2(127.0 - byte)[:, None, :]).reshape(k, n).astype(np.float32)
    by_word = np.ascontiguousarray(scaled.reshape(k // 512, 128, 4, n).transpose(0, 1, 3, 2))
    if fmt == "e4m3":
        words = by_word.astype(ml_dtypes.float8_e4m3fn).view(np.uint8)
    else:
        c = by_word.astype(ml_dtypes.float4_e2m1fn).view(np.uint8) & 0xF
        words = (c[..., 0::2] | (c[..., 1::2] << 4)).reshape(k // 512, 128, 2 * n)
    return np.ascontiguousarray(words), np.ascontiguousarray(byte.astype(np.uint8).reshape(k // 512, 16, n))


def unpack_weight(words, scales, fmt):
    g, _, n = scales.shape
    words = np.ascontiguousarray(words).reshape(g, 128, n, -1)
    if fmt == "e4m3":
        vals = words.view(ml_dtypes.float8_e4m3fn).astype(np.float64)
    else:
        nib = np.empty((g, 128, n, 4), np.uint8)
        nib[..., 0::2] = words & 0xF
        nib[..., 1::2] = words >> 4
        vals = E2M1[nib]
    vals = vals * np.repeat(np.exp2(scales.astype(np.float64) - 127.0), 8, axis=1)[..., None]
    return vals.transpose(0, 1, 3, 2).reshape(g * 512, n)


K, T, J, N = 512, 512, 512, 512


def setup_inputs():
    n = np.random.standard_normal
    idx = np.random.randint(0, T, J)
    idx2 = np.random.randint(0, T, J)
    fk = mx_kscale(K)
    wap = pack_weight(n((K, N)) * 1 / np.sqrt(K) * fk[:, None], "e2m1")
    wbp = pack_weight(n((K, N)) * 1 / np.sqrt(K) * fk[:, None], "e4m3")
    return {
        "xt": (n((K, T)) / fk[:, None]).astype(np.float32),
        "wa_words": wap[0],
        "wa_scales": wap[1],
        "wb_words": wbp[0],
        "wb_scales": wbp[1],
        "offs": striped(idx),
        "offs2": striped(idx2),
    }


def reference(xt, wa_words, wa_scales, wb_words, wb_scales, offs, offs2):
    idx = unstriped(offs)
    idx2 = unstriped(offs2)
    wau = unpack_weight(wa_words, wa_scales, "e2m1")
    wbu = unpack_weight(wb_words, wb_scales, "e4m3")
    xtq = mxq(f64(xt), 0, "e4m3")
    za = wau.T @ xtq
    zb = wbu.T @ xtq
    m1 = np.maximum(za[:, idx], zb[:, idx2])
    d = np.abs(za[:, idx] - zb[:, idx2])
    y = m1 + np.log(1.0 + np.exp(0.0 - d))
    return y

@@ -1,0 +1,158 @@
+from contextlib import ExitStack
+
+import concourse.mybir as mybir
+
+K, T, J, N = 512, 512, 512, 512
+FLOPS = 2 * 2 * K * T * N
+
+F32 = mybir.dt.float32
+BF16 = mybir.dt.bfloat16
+I32 = mybir.dt.int32
+U32 = mybir.dt.uint32
+U16 = mybir.dt.uint16
+U8 = mybir.dt.uint8
+FP8X4 = mybir.dt.float8_e4m3fn_x4
+FP4X4 = mybir.dt.float4_e2m1fn_x4
+ACT = mybir.ActivationFunctionType
+ALU = mybir.AluOpType
+
+P = 128
+PACK = 4
+ROW_TILES = N // P
+TOKEN_CHUNKS = (256, 256,)
+SCALAR_TOKENS = (80, 80,)
+A_PIECES = (256, 256)
+B_PIECES = ((256, 256,), (256, 256,), (256, 256,), (256, 128, 128,),)
+LN_PIECES = ((256, 256,), (512,), (512,), (256, 256,),)
+
+
+def spans(widths):
+    return [slice(sum(widths[:i]), sum(widths[: i + 1])) for i in range(len(widths))]
+
+
+def entries(span):
+    return slice(span.start // 16, span.stop // 16)
+
+
+def tile_list_smooth_larger_of_two_kernel(tc, xt, wa_words, wa_scales, wb_words, wb_scales, offs, offs2, out):
+    nc = tc.nc
+    with ExitStack() as ctx:
+        lists = ctx.enter_context(tc.tile_pool(name="lists", bufs=1))
+        keep = ctx.enter_context(tc.tile_pool(name="keep", bufs=1))
+        psum = ctx.enter_context(tc.psum_pool(name="psum", bufs=1))
+
+        chunks = spans(TOKEN_CHUNKS)
+        w_scales = keep.tile([P, 2 * N], U8, name="w_scales", align_bytes=64)
+        nc.gpsimd.memset(w_scales[:].bitcast(U32), 0)
+        sa = w_scales[:, 0:N]
+        sb = w_scales[:, N : 2 * N]
+        for q in range(4):
+            nc.scalar.dma_start(out=sa[32 * q : 32 * q + 4, :].bitcast(I32), in_=wa_scales[0, 4 * q : 4 * q + 4, :].bitcast(I32))
+        x_rows = xt.rearrange("(p r) t -> p r t", r=PACK)
+        raw = []
+        wa = keep.tile([P, 2 * N], U8, name="wa", align_bytes=64)
+        wb = keep.tile([P, N], U32, name="wb", align_bytes=64)
+        for c, width in enumerate(TOKEN_CHUNKS):
+            tile = keep.tile([P, PACK, width], F32, name="raw%d" % c)
+            nc.sync.dma_start(out=tile[:], in_=x_rows[:, :, chunks[c]])
+            raw.append(tile)
+            if c == 0:
+                nc.sync.dma_start(out=wa[:].bitcast(I32), in_=wa_words[0].bitcast(I32))
+        nc.sync.dma_start(out=wb[:].bitcast(I32), in_=wb_words[0].rearrange("p n r -> p (n r)").bitcast(I32))
+        for q in range(4):
+            nc.sync.dma_start(out=sb[32 * q : 32 * q + 4, :].bitcast(I32), in_=wb_scales[0, 4 * q : 4 * q + 4, :].bitcast(I32))
+        list_a = lists.tile([P, J // 16], U16, name="list_a")
+        list_b = lists.tile([P, J // 16], U16, name="list_b")
+        nc.sync.dma_start(list_a[:], offs)
+        nc.sync.dma_start(list_b[:], offs2)
+
+        codes = keep.tile([P, T], U32, name="codes", align_bytes=64)
+        scales = keep.tile([P, T], U8, name="scales", align_bytes=64)
+        for c, width in enumerate(TOKEN_CHUNKS):
+            grouped = keep.tile([P, width, PACK], BF16, name="grouped%d" % c, align_bytes=64)
+            cut = width - SCALAR_TOKENS[c]
+            nc.vector.tensor_copy(
+                out=grouped[:, 0:cut, :].rearrange("p (g i) r -> p g r i", i=4),
+                in_=raw[c][:, :, 0:cut].rearrange("p r (g i) -> p g r i", i=4),
+            )
+            if cut < width:
+                nc.scalar.activation(
+                    out=grouped[:, cut:width, :].rearrange("p (g i) r -> p g r i", i=4),
+                    in_=raw[c][:, :, cut:width].rearrange("p r (g i) -> p g r i", i=4),
+                    func=ACT.Copy,
+                )
+            nc.vector.quantize_mx(
+                out=codes[:, chunks[c]].bitcast(FP8X4), scales=scales[:, chunks[c]], in_=grouped[:].rearrange("p t r -> p (t r)")
+            )
+
+        def product(dst, second, m, tokens):
+            words = wb[:, P * m : P * (m + 1)].bitcast(FP8X4) if second else wa[:, 2 * P * m : 2 * P * (m + 1)].bitcast(FP4X4)
+            plane = sb if second else sa
+            nc.tensor.matmul_mx(
+                out=dst,
+                lhsT=words,
+                lhsT_scale=plane[:, P * m : P * (m + 1)],
+                rhs=codes[:, tokens].bitcast(FP8X4),
+                rhs_scale=scales[:, tokens],
+                start=True,
+                stop=True,
+            )
+
+        last = ROW_TILES - 1
+        za, zb = [], []
+        for m in range(ROW_TILES):
+            win_a = keep.tile([P, T], F32, name="za%d" % m)
+            win_b = keep.tile([P, T], F32, name="zb%d" % m, tag="after_gathers" if m == last else "zb%d" % m)
+            if m == 0:
+                for c, tokens in enumerate(chunks):
+                    part = psum.tile([P, TOKEN_CHUNKS[c]], F32, name="part%d" % c, tag="part%d" % c)
+                    product(part[:], False, m, tokens)
+                    if c == len(chunks) - 1:
+                        nc.vector.tensor_copy(out=win_a[:, tokens], in_=part[:])
+                    else:
+                        nc.scalar.activation(out=win_a[:, tokens], in_=part[:], func=ACT.Copy)
+            else:
+                bank_a = psum.tile([P, T], F32, name="bank_a%d" % m)
+                product(bank_a[:], False, m, slice(0, T))
+                nc.scalar.activation(out=win_a[:], in_=bank_a[:], func=ACT.Copy)
+            bank_b = psum.tile([P, T], F32, name="bank_b%d" % m, tag="part0" if m == last else "bank_b%d" % m)
+            product(bank_b[:], True, m, slice(0, T))
+            nc.scalar.activation(out=win_b[:], in_=bank_b[:], func=ACT.Copy)
+            za.append(win_a)
+            zb.append(win_b)
+
+        picked, gap, size = [], [], []
+        for m in range(ROW_TILES):
+            a = keep.tile([P, J], F32, name="picked%d" % m)
+            d = keep.tile([P, J], F32, name="gap%d" % m)
+            s = keep.tile([P, J], F32, name="size%d" % m)
+            for slots in spans(A_PIECES):
+                nc.vector.tensor_copy(out=a[:, slots], in_=za[m][:].indirect(list_a[:, entries(slots)]))
+            for slots in spans(B_PIECES[m]):
+                nc.vector.tensor_tensor(out=d[:, slots], in0=zb[m][:].indirect(list_b[:, entries(slots)]), in1=a[:, slots], op=ALU.subtract)
+            for slots in spans(B_PIECES[m]):
+                is_last = m == last and slots.stop == J
+                tag = "after_tanh" if is_last else "th%d_%d" % (m, slots.start)
+                th = keep.tile([P, slots.stop - slots.start], F32, name="th%d_%d" % (m, slots.start), tag=tag)
+                nc.scalar.activation(out=th[:], in_=d[:, slots], func=ACT.Tanh, scale=0.5)
+                if is_last:
+                    nc.vector.scalar_tensor_tensor(out=s[:, slots], in0=th[:], scalar=-1.0, in1=th[:], op0=ALU.mult, op1=ALU.max)
+                else:
+                    nc.scalar.activation(out=s[:, slots], in_=th[:], func=ACT.Abs)
+            picked.append(a)
+            gap.append(d)
+            size.append(s)
+
+        larger = keep.tile([P, ROW_TILES * J], F32, name="larger", tag="after_gathers")
+        bonus = keep.tile([P, ROW_TILES * J], F32, name="bonus", tag="after_tanh")
+        for m in range(ROW_TILES):
+            nc.vector.scalar_tensor_tensor(
+                out=larger[:, m * J : (m + 1) * J], in0=gap[m][:], scalar=0.0, in1=picked[m][:], op0=ALU.max, op1=ALU.add
+            )
+        for m in range(ROW_TILES):
+            for slots in spans(LN_PIECES[m]):
+                wide = slice(m * J + slots.start, m * J + slots.stop)
+                nc.scalar.activation(out=bonus[:, wide], in_=size[m][:, slots], func=ACT.Ln, bias=0.5, scale=0.5)
+                result = keep.tile([P, slots.stop - slots.start], F32, name="result%d_%d" % (m, slots.start))
+                nc.vector.tensor_tensor(out=result[:], in0=larger[:, wide], in1=bonus[:, wide], op=ALU.subtract)
+                nc.sync.dma_start(out=out[m * P : (m + 1) * P, slots], in_=result[:])

@@ -23,7 +23,8 @@ TOKEN_CHUNKS = (256, 256,)
 SCALAR_TOKENS = (80, 80,)
 A_PIECES = (256, 256)
 B_PIECES = ((256, 256,), (256, 256,), (256, 256,), (256, 128, 128,),)
-LN_PIECES = ((256, 256,), (512,), (512,), (256, 256,),)
+LN_PIECES = ((256, 256,), (256, 256,), (256, 256,), (256, 256,),)
+ORDER = "a0 a1 b0 b1 a2 b2 a3 b3".split()
 
 
 def spans(widths):
@@ -42,28 +43,27 @@ def tile_list_smooth_larger_of_two_kernel(tc, xt, wa_words, wa_scales, wb_words,
         psum = ctx.enter_context(tc.psum_pool(name="psum", bufs=1))
 
         chunks = spans(TOKEN_CHUNKS)
-        w_scales = keep.tile([P, 2 * N], U8, name="w_scales", align_bytes=64)
-        nc.gpsimd.memset(w_scales[:].bitcast(U32), 0)
-        sa = w_scales[:, 0:N]
-        sb = w_scales[:, N : 2 * N]
-        for q in range(4):
-            nc.scalar.dma_start(out=sa[32 * q : 32 * q + 4, :].bitcast(I32), in_=wa_scales[0, 4 * q : 4 * q + 4, :].bitcast(I32))
+        sa = keep.tile([P, N], U8, name="sa", align_bytes=64)
+        sb = keep.tile([P, N], U8, name="sb", align_bytes=64)
+        nc.vector.memset(sa[:].bitcast(U32), 0)
+        nc.vector.memset(sb[:].bitcast(U32), 0)
         x_rows = xt.rearrange("(p r) t -> p r t", r=PACK)
         raw = []
-        wa = keep.tile([P, 2 * N], U8, name="wa", align_bytes=64)
-        wb = keep.tile([P, N], U32, name="wb", align_bytes=64)
         for c, width in enumerate(TOKEN_CHUNKS):
             tile = keep.tile([P, PACK, width], F32, name="raw%d" % c)
             nc.sync.dma_start(out=tile[:], in_=x_rows[:, :, chunks[c]])
             raw.append(tile)
-            if c == 0:
-                nc.sync.dma_start(out=wa[:].bitcast(I32), in_=wa_words[0].bitcast(I32))
+        wa = keep.tile([P, 2 * N], U8, name="wa", align_bytes=64)
+        wb = keep.tile([P, N], U32, name="wb", align_bytes=64)
+        list_a = lists.tile([P, J // 16], U16, name="list_a")
+        list_b = lists.tile([P, J // 16], U16, name="list_b")
+        nc.sync.dma_start(out=wa[:].bitcast(I32), in_=wa_words[0].bitcast(I32))
+        for q in range(4):
+            nc.sync.dma_start(out=sa[32 * q : 32 * q + 4, :].bitcast(I32), in_=wa_scales[0, 4 * q : 4 * q + 4, :].bitcast(I32))
+        nc.sync.dma_start(list_a[:], offs)
         nc.sync.dma_start(out=wb[:].bitcast(I32), in_=wb_words[0].rearrange("p n r -> p (n r)").bitcast(I32))
         for q in range(4):
             nc.sync.dma_start(out=sb[32 * q : 32 * q + 4, :].bitcast(I32), in_=wb_scales[0, 4 * q : 4 * q + 4, :].bitcast(I32))
-        list_a = lists.tile([P, J // 16], U16, name="list_a")
-        list_b = lists.tile([P, J // 16], U16, name="list_b")
-        nc.sync.dma_start(list_a[:], offs)
         nc.sync.dma_start(list_b[:], offs2)
 
         codes = keep.tile([P, T], U32, name="codes", align_bytes=64)
@@ -99,56 +99,61 @@ def tile_list_smooth_larger_of_two_kernel(tc, xt, wa_words, wa_scales, wb_words,
             )
 
         last = ROW_TILES - 1
-        za, zb = [], []
-        for m in range(ROW_TILES):
-            win_a = keep.tile([P, T], F32, name="za%d" % m)
-            win_b = keep.tile([P, T], F32, name="zb%d" % m, tag="after_gathers" if m == last else "zb%d" % m)
-            if m == 0:
+        window = {}
+        for step, key in enumerate(ORDER):
+            m = int(key[1])
+            win = keep.tile([P, T], F32, name="z" + key, tag="after_gathers" if key == ORDER[-1] else "z" + key)
+            if step == 0:
                 for c, tokens in enumerate(chunks):
                     part = psum.tile([P, TOKEN_CHUNKS[c]], F32, name="part%d" % c, tag="part%d" % c)
                     product(part[:], False, m, tokens)
                     if c == len(chunks) - 1:
-                        nc.vector.tensor_copy(out=win_a[:, tokens], in_=part[:])
+                        nc.vector.tensor_copy(out=win[:, tokens], in_=part[:])
                     else:
-                        nc.scalar.activation(out=win_a[:, tokens], in_=part[:], func=ACT.Copy)
+                        nc.scalar.activation(out=win[:, tokens], in_=part[:], func=ACT.Copy)
             else:
-                bank_a = psum.tile([P, T], F32, name="bank_a%d" % m)
-                product(bank_a[:], False, m, slice(0, T))
-                nc.scalar.activation(out=win_a[:], in_=bank_a[:], func=ACT.Copy)
-            bank_b = psum.tile([P, T], F32, name="bank_b%d" % m, tag="part0" if m == last else "bank_b%d" % m)
-            product(bank_b[:], True, m, slice(0, T))
-            nc.scalar.activation(out=win_b[:], in_=bank_b[:], func=ACT.Copy)
-            za.append(win_a)
-            zb.append(win_b)
+                held = key[0] == "a" and m >= 2
+                bank = psum.tile([P, T], F32, name="bank" + key, tag="bankb%d" % (m - 2) if held else "bank" + key)
+                product(bank[:], key[0] == "b", m, slice(0, T))
+                nc.scalar.activation(out=win[:], in_=bank[:], func=ACT.Copy)
+            window[key] = win
 
-        picked, gap, size = [], [], []
-        for m in range(ROW_TILES):
-            a = keep.tile([P, J], F32, name="picked%d" % m)
+        picked, other, gap, size = {}, {}, {}, {}
+        for key in ORDER:
+            m = int(key[1])
+            if key[0] == "a":
+                a = keep.tile([P, J], F32, name="picked%d" % m, tag="zb%d" % (m - 2) if m >= 2 else "picked%d" % m)
+                for slots in spans(A_PIECES):
+                    nc.vector.tensor_copy(out=a[:, slots], in_=window[key][:].indirect(list_a[:, entries(slots)]))
+                picked[m] = a
+                continue
+            a = picked[m]
             d = keep.tile([P, J], F32, name="gap%d" % m)
             s = keep.tile([P, J], F32, name="size%d" % m)
-            for slots in spans(A_PIECES):
-                nc.vector.tensor_copy(out=a[:, slots], in_=za[m][:].indirect(list_a[:, entries(slots)]))
             for slots in spans(B_PIECES[m]):
-                nc.vector.tensor_tensor(out=d[:, slots], in0=zb[m][:].indirect(list_b[:, entries(slots)]), in1=a[:, slots], op=ALU.subtract)
+                nc.vector.tensor_tensor(out=d[:, slots], in0=window[key][:].indirect(list_b[:, entries(slots)]), in1=a[:, slots], op=ALU.subtract)
             for slots in spans(B_PIECES[m]):
                 is_last = m == last and slots.stop == J
                 tag = "after_tanh" if is_last else "th%d_%d" % (m, slots.start)
                 th = keep.tile([P, slots.stop - slots.start], F32, name="th%d_%d" % (m, slots.start), tag=tag)
                 nc.scalar.activation(out=th[:], in_=d[:, slots], func=ACT.Tanh, scale=0.5)
                 if is_last:
-                    nc.vector.scalar_tensor_tensor(out=s[:, slots], in0=th[:], scalar=-1.0, in1=th[:], op0=ALU.mult, op1=ALU.max)
+                    final_th, final_slots = th, slots
                 else:
                     nc.scalar.activation(out=s[:, slots], in_=th[:], func=ACT.Abs)
-            picked.append(a)
-            gap.append(d)
-            size.append(s)
+            gap[m] = d
+            size[m] = s
 
         larger = keep.tile([P, ROW_TILES * J], F32, name="larger", tag="after_gathers")
-        bonus = keep.tile([P, ROW_TILES * J], F32, name="bonus", tag="after_tanh")
         for m in range(ROW_TILES):
             nc.vector.scalar_tensor_tensor(
                 out=larger[:, m * J : (m + 1) * J], in0=gap[m][:], scalar=0.0, in1=picked[m][:], op0=ALU.max, op1=ALU.add
             )
+            if m == 0:
+                nc.vector.scalar_tensor_tensor(
+                    out=size[last][:, final_slots], in0=final_th[:], scalar=-1.0, in1=final_th[:], op0=ALU.mult, op1=ALU.max
+                )
+        bonus = keep.tile([P, ROW_TILES * J], F32, name="bonus", tag="after_tanh")
         for m in range(ROW_TILES):
             for slots in spans(LN_PIECES[m]):
                 wide = slice(m * J + slots.start, m * J + slots.stop)

@@ -23,7 +23,7 @@ TOKEN_CHUNKS = (256, 256,)
 SCALAR_TOKENS = (80, 80,)
 A_PIECES = (256, 256)
 B_PIECES = ((256, 256,), (256, 256,), (256, 256,), (256, 128, 128,),)
-LN_PIECES = ((256, 256,), (256, 256,), (256, 256,), (256, 256,),)
+LN_PIECES = ((128, 128, 256,), (256, 256,), (256, 256,), (256, 256,),)
 ORDER = "a0 a1 b0 b1 a2 b2 a3 b3".split()
 
 
@@ -61,10 +61,10 @@ def tile_list_smooth_larger_of_two_kernel(tc, xt, wa_words, wa_scales, wb_words,
         for q in range(4):
             nc.sync.dma_start(out=sa[32 * q : 32 * q + 4, :].bitcast(I32), in_=wa_scales[0, 4 * q : 4 * q + 4, :].bitcast(I32))
         nc.sync.dma_start(list_a[:], offs)
+        nc.sync.dma_start(list_b[:], offs2)
         nc.sync.dma_start(out=wb[:].bitcast(I32), in_=wb_words[0].rearrange("p n r -> p (n r)").bitcast(I32))
         for q in range(4):
             nc.sync.dma_start(out=sb[32 * q : 32 * q + 4, :].bitcast(I32), in_=wb_scales[0, 4 * q : 4 * q + 4, :].bitcast(I32))
-        nc.sync.dma_start(list_b[:], offs2)
 
         codes = keep.tile([P, T], U32, name="codes", align_bytes=64)
         scales = keep.tile([P, T], U8, name="scales", align_bytes=64)

from contextlib import ExitStack

import concourse.mybir as mybir

K, T, J, N = 512, 512, 512, 512
FLOPS = 2 * 2 * K * T * N

F32 = mybir.dt.float32
BF16 = mybir.dt.bfloat16
I32 = mybir.dt.int32
U32 = mybir.dt.uint32
U16 = mybir.dt.uint16
U8 = mybir.dt.uint8
FP8X4 = mybir.dt.float8_e4m3fn_x4
FP4X4 = mybir.dt.float4_e2m1fn_x4
ACT = mybir.ActivationFunctionType
ALU = mybir.AluOpType

P = 128
PACK = 4
ROW_TILES = N // P
TOKEN_CHUNKS = (256, 256,)
SCALAR_TOKENS = (80, 80,)
A_PIECES = (256, 256)
B_PIECES = ((256, 256,), (256, 256,), (256, 256,), (256, 128, 128,),)
LN_PIECES = ((128, 128, 256,), (256, 256,), (256, 256,), (256, 256,),)
ORDER = "a0 a1 b0 b1 a2 b2 a3 b3".split()


def spans(widths):
    return [slice(sum(widths[:i]), sum(widths[: i + 1])) for i in range(len(widths))]


def entries(span):
    return slice(span.start // 16, span.stop // 16)


def tile_list_smooth_larger_of_two_kernel(tc, xt, wa_words, wa_scales, wb_words, wb_scales, offs, offs2, out):
    nc = tc.nc
    with ExitStack() as ctx:
        lists = ctx.enter_context(tc.tile_pool(name="lists", bufs=1))
        keep = ctx.enter_context(tc.tile_pool(name="keep", bufs=1))
        psum = ctx.enter_context(tc.psum_pool(name="psum", bufs=1))

        chunks = spans(TOKEN_CHUNKS)
        sa = keep.tile([P, N], U8, name="sa", align_bytes=64)
        sb = keep.tile([P, N], U8, name="sb", align_bytes=64)
        nc.vector.memset(sa[:].bitcast(U32), 0)
        nc.vector.memset(sb[:].bitcast(U32), 0)
        x_rows = xt.rearrange("(p r) t -> p r t", r=PACK)
        raw = []
        for c, width in enumerate(TOKEN_CHUNKS):
            tile = keep.tile([P, PACK, width], F32, name="raw%d" % c)
            nc.sync.dma_start(out=tile[:], in_=x_rows[:, :, chunks[c]])
            raw.append(tile)
        wa = keep.tile([P, 2 * N], U8, name="wa", align_bytes=64)
        wb = keep.tile([P, N], U32, name="wb", align_bytes=64)
        list_a = lists.tile([P, J // 16], U16, name="list_a")
        list_b = lists.tile([P, J // 16], U16, name="list_b")
        nc.sync.dma_start(out=wa[:].bitcast(I32), in_=wa_words[0].bitcast(I32))
        for q in range(4):
            nc.sync.dma_start(out=sa[32 * q : 32 * q + 4, :].bitcast(I32), in_=wa_scales[0, 4 * q : 4 * q + 4, :].bitcast(I32))
        nc.sync.dma_start(list_a[:], offs)
        nc.sync.dma_start(list_b[:], offs2)
        nc.sync.dma_start(out=wb[:].bitcast(I32), in_=wb_words[0].rearrange("p n r -> p (n r)").bitcast(I32))
        for q in range(4):
            nc.sync.dma_start(out=sb[32 * q : 32 * q + 4, :].bitcast(I32), in_=wb_scales[0, 4 * q : 4 * q + 4, :].bitcast(I32))

        codes = keep.tile([P, T], U32, name="codes", align_bytes=64)
        scales = keep.tile([P, T], U8, name="scales", align_bytes=64)
        for c, width in enumerate(TOKEN_CHUNKS):
            grouped = keep.tile([P, width, PACK], BF16, name="grouped%d" % c, align_bytes=64)
            cut = width - SCALAR_TOKENS[c]
            nc.vector.tensor_copy(
                out=grouped[:, 0:cut, :].rearrange("p (g i) r -> p g r i", i=4),
                in_=raw[c][:, :, 0:cut].rearrange("p r (g i) -> p g r i", i=4),
            )
            if cut < width:
                nc.scalar.activation(
                    out=grouped[:, cut:width, :].rearrange("p (g i) r -> p g r i", i=4),
                    in_=raw[c][:, :, cut:width].rearrange("p r (g i) -> p g r i", i=4),
                    func=ACT.Copy,
                )
            nc.vector.quantize_mx(
                out=codes[:, chunks[c]].bitcast(FP8X4), scales=scales[:, chunks[c]], in_=grouped[:].rearrange("p t r -> p (t r)")
            )

        def product(dst, second, m, tokens):
            words = wb[:, P * m : P * (m + 1)].bitcast(FP8X4) if second else wa[:, 2 * P * m : 2 * P * (m + 1)].bitcast(FP4X4)
            plane = sb if second else sa
            nc.tensor.matmul_mx(
                out=dst,
                lhsT=words,
                lhsT_scale=plane[:, P * m : P * (m + 1)],
                rhs=codes[:, tokens].bitcast(FP8X4),
                rhs_scale=scales[:, tokens],
                start=True,
                stop=True,
            )

        last = ROW_TILES - 1
        window = {}
        for step, key in enumerate(ORDER):
            m = int(key[1])
            win = keep.tile([P, T], F32, name="z" + key, tag="after_gathers" if key == ORDER[-1] else "z" + key)
            if step == 0:
                for c, tokens in enumerate(chunks):
                    part = psum.tile([P, TOKEN_CHUNKS[c]], F32, name="part%d" % c, tag="part%d" % c)
                    product(part[:], False, m, tokens)
                    if c == len(chunks) - 1:
                        nc.vector.tensor_copy(out=win[:, tokens], in_=part[:])
                    else:
                        nc.scalar.activation(out=win[:, tokens], in_=part[:], func=ACT.Copy)
            else:
                held = key[0] == "a" and m >= 2
                bank = psum.tile([P, T], F32, name="bank" + key, tag="bankb%d" % (m - 2) if held else "bank" + key)
                product(bank[:], key[0] == "b", m, slice(0, T))
                nc.scalar.activation(out=win[:], in_=bank[:], func=ACT.Copy)
            window[key] = win

        picked, other, gap, size = {}, {}, {}, {}
        for key in ORDER:
            m = int(key[1])
            if key[0] == "a":
                a = keep.tile([P, J], F32, name="picked%d" % m, tag="zb%d" % (m - 2) if m >= 2 else "picked%d" % m)
                for slots in spans(A_PIECES):
                    nc.vector.tensor_copy(out=a[:, slots], in_=window[key][:].indirect(list_a[:, entries(slots)]))
                picked[m] = a
                continue
            a = picked[m]
            d = keep.tile([P, J], F32, name="gap%d" % m)
            s = keep.tile([P, J], F32, name="size%d" % m)
            for slots in spans(B_PIECES[m]):
                nc.vector.tensor_tensor(out=d[:, slots], in0=window[key][:].indirect(list_b[:, entries(slots)]), in1=a[:, slots], op=ALU.subtract)
            for slots in spans(B_PIECES[m]):
                is_last = m == last and slots.stop == J
                tag = "after_tanh" if is_last else "th%d_%d" % (m, slots.start)
                th = keep.tile([P, slots.stop - slots.start], F32, name="th%d_%d" % (m, slots.start), tag=tag)
                nc.scalar.activation(out=th[:], in_=d[:, slots], func=ACT.Tanh, scale=0.5)
                if is_last:
                    final_th, final_slots = th, slots
                else:
                    nc.scalar.activation(out=s[:, slots], in_=th[:], func=ACT.Abs)
            gap[m] = d
            size[m] = s

        larger = keep.tile([P, ROW_TILES * J], F32, name="larger", tag="after_gathers")
        for m in range(ROW_TILES):
            nc.vector.scalar_tensor_tensor(
                out=larger[:, m * J : (m + 1) * J], in0=gap[m][:], scalar=0.0, in1=picked[m][:], op0=ALU.max, op1=ALU.add
            )
            if m == 0:
                nc.vector.scalar_tensor_tensor(
                    out=size[last][:, final_slots], in0=final_th[:], scalar=-1.0, in1=final_th[:], op0=ALU.mult, op1=ALU.max
                )
        bonus = keep.tile([P, ROW_TILES * J], F32, name="bonus", tag="after_tanh")
        for m in range(ROW_TILES):
            for slots in spans(LN_PIECES[m]):
                wide = slice(m * J + slots.start, m * J + slots.stop)
                nc.scalar.activation(out=bonus[:, wide], in_=size[m][:, slots], func=ACT.Ln, bias=0.5, scale=0.5)
                result = keep.tile([P, slots.stop - slots.start], F32, name="result%d_%d" % (m, slots.start))
                nc.vector.tensor_tensor(out=result[:], in0=larger[:, wide], in1=bonus[:, wide], op=ALU.subtract)
                nc.sync.dma_start(out=out[m * P : (m + 1) * P, slots], in_=result[:])
